import numpy as np
import ml_dtypes


def mxq(x, axis, fmt="e4m3"):
    dtype, down = {"e4m3": (ml_dtypes.float8_e4m3fn, 7), "e5m2": (ml_dtypes.float8_e5m2, 14)}[fmt]
    v = np.moveaxis(np.asarray(x, np.float32).astype(ml_dtypes.bfloat16).astype(np.float64), axis, -1)
    blocks = v.reshape(v.shape[:-1] + (-1, 32))
    amax = np.abs(blocks).max(-1, keepdims=True)
    byte = np.maximum(np.where(amax > 0, np.frexp(amax)[1] - 1 + 127, 0) - down, 1)
    scale = np.exp2(byte - 127.0)
    codes = (blocks / scale).astype(np.float32).astype(dtype).astype(np.float64)
    return np.moveaxis((codes * scale).reshape(v.shape), -1, axis)


WIDE = False


def mx_kscale(k):
    if not WIDE:
        return np.ones(k)
    levels = np.array([10, -10, 5, -5, 0])
    if k % 512:
        return np.exp2(np.random.permutation(np.resize(levels, k // 32))).repeat(32)
    a = np.empty((k // 512, 16))
    for p in range(k // 512):
        a[p, :8] = np.random.permutation(np.resize(levels, 8))
        for g in range(8):
            far = levels[np.abs(levels - a[p, g]) >= 10]
            a[p, g + 8] = far[np.random.randint(len(far))]
    return np.exp2(a.ravel()).repeat(32)


def f64(x):
    return np.asarray(x).astype(np.float64)


def striped(idx):
    return np.tile(idx.reshape(-1, 16).T, (8, 1)).astype(np.uint16)


def unstriped(offs):
    return offs[:16].T.reshape(-1).astype(np.int64)


def striped8(idx):
    return np.concatenate([x.reshape(-1, 16).T for x in idx]).astype(np.uint16)


def runs(offs, k):
    lists = np.stack([offs[16 * r : 16 * r + 16].T.reshape(-1) for r in range(8)]).astype(np.int64)
    return lists[np.arange(k) % 512 // 64]


def pack_weight(w):
    k, n = w.shape
    w = f64(np.asarray(w, np.float32).astype(ml_dtypes.bfloat16)).reshape(k // 32, 32, n)
    amax = np.abs(w).max(1)
    byte = np.clip(np.where(amax > 0, np.frexp(amax)[1] - 1 + 127 - 7, 1), 1, 254)
    scaled = (w * np.exp2(127.0 - byte)[:, None, :]).reshape(k, n).astype(np.float32)
    words = np.ascontiguousarray(scaled.reshape(k // 512, 128, 4, n).transpose(0, 1, 3, 2)).astype(ml_dtypes.float8_e4m3fn).view(np.uint8)
    return words, np.ascontiguousarray(byte.astype(np.uint8).reshape(k // 512, 16, n))


def unpack_weight(words, scales):
    g, p, n, _ = words.shape
    vals = np.ascontiguousarray(words).view(ml_dtypes.float8_e4m3fn).astype(np.float64) * np.repeat(np.exp2(scales.astype(np.float64) - 127.0), 8, axis=1)[..., None]
    return vals.transpose(0, 1, 3, 2).reshape(g * 512, n)


K, T, S, H, G, W = 512, 2048, 256, 512, 2048, 128


def setup_inputs():
    n = np.random.standard_normal
    s = mx_kscale(K)[:, None]
    packed_xT = pack_weight(n((K, T)) * s)
    packed_dT = pack_weight(n((K, G)) / s)
    perm = np.random.permutation(S)
    return {
        "x_words": packed_xT[0],
        "x_scales": packed_xT[1],
        "w1": (n((K, H)) / np.sqrt(K) / s).astype(np.float32),
        "gs": (np.random.uniform(0.5, 1.5, (K, 1)) * s).astype(np.float32),
        "d_words": packed_dT[0],
        "d_scales": packed_dT[1],
        "offs": striped(np.random.permutation(T)[:S]),
        "n1": striped8(np.stack([np.random.permutation(S) for _ in range(8)])),
        "n2": striped8(np.stack([np.random.permutation(S) for _ in range(8)])),
        "k1": striped8(np.random.randint(0, G, (8, H))),
        "n3": striped(perm[:W]),
        "n4": striped(perm[W:]),
    }


def reference(x_words, x_scales, w1, gs, d_words, d_scales, offs, n1, n2, k1, n3, n4):
    d_k1 = unpack_weight(d_words, d_scales)[np.arange(K)[:, None], runs(k1, K)]
    xq = unpack_weight(x_words, x_scales)[:, unstriped(offs)]
    y = mxq(f64(w1), 0, "e4m3").T @ xq
    st = np.maximum(y, y[np.arange(H)[:, None], runs(n1, H)])
    z = f64(gs) * (np.minimum(st, st[np.arange(H)[:, None], runs(n2, H)]))
    h = 0.0625 * ((d_k1.T @ mxq(z, 0, "e4m3")))
    pb = h[:, unstriped(n4)]
    pa = h[:, unstriped(n3)]
    rb = pb - (0.5 * pa)
    ra = np.sqrt((pa) ** 2 + (pb) ** 2 + 0.25)
    ds = np.zeros((H, S))
    ds[:, unstriped(n3)] = ra
    out = ds.copy()
    out[:, unstriped(n4)] = rb
    return out

@@ -1,0 +1,215 @@
+from contextlib import ExitStack
+
+import concourse.mybir as mybir
+
+K, T, S, H, G, W = 512, 2048, 256, 512, 2048, 128
+FLOPS = 2 * K * H * S + 2 * H * H * S
+
+F32 = mybir.dt.float32
+BF16 = mybir.dt.bfloat16
+I32 = mybir.dt.int32
+U32 = mybir.dt.uint32
+U16 = mybir.dt.uint16
+U8 = mybir.dt.uint8
+FP8X4 = mybir.dt.float8_e4m3fn_x4
+ALU = mybir.AluOpType
+ACT = mybir.ActivationFunctionType
+
+P = 128
+PACK = 4
+PIECE = 64
+HALF = S // 2
+
+
+def tile_picked_densehopmnpolar_none_p_kernel(
+    tc, x_words, x_scales, w1, gs, d_words, d_scales, offs, n1, n2, k1, n3, n4, out
+):
+    nc = tc.nc
+    with ExitStack() as ctx:
+        keep = ctx.enter_context(tc.tile_pool(name="keep", bufs=1))
+        psum = ctx.enter_context(tc.psum_pool(name="psum", bufs=1))
+
+        def tile(name, cols, dtype, tag=None):
+            return keep.tile([P, cols], dtype, name=name, tag=tag or name, align_bytes=64)
+
+        def load_list(name, src):
+            held = keep.tile([P, src.shape[1]], U16, name=name)
+            nc.sync.dma_start(held[:], src)
+            return held
+
+        xs_table = tile("xs_table", T, U8)
+        nc.vector.memset(xs_table[:].bitcast(I32), 0)
+        ds_table = tile("ds_table", G, U8)
+        nc.vector.memset(ds_table[:].bitcast(I32), 0)
+
+        offs_sb = load_list("offs_sb", offs)
+        w_raw = tile("w_raw", PACK * H, F32, tag="big")
+        nc.scalar.dma_start(w_raw[:], w1.rearrange("(p j) c -> p (j c)", j=PACK))
+        x_table = tile("x_table", T, I32)
+        nc.scalar.dma_start(x_table[:], x_words[0].rearrange("p n t -> p (n t)").bitcast(I32))
+        for q in range(4):
+            nc.sync.dma_start(xs_table[32 * q : 32 * q + 4, :].bitcast(I32), x_scales[0, 4 * q : 4 * q + 4, :].bitcast(I32))
+        gain = tile("gain", PACK, F32)
+        nc.sync.dma_start(gain[:], gs.rearrange("(p t) o -> p (t o)", t=PACK))
+        k1_sb = load_list("k1_sb", k1)
+        nc.sync.dma_start(ds_table[0:P:8, :].bitcast(I32), d_scales[0].bitcast(I32))
+        n1_sb = load_list("n1_sb", n1)
+        n2_sb = load_list("n2_sb", n2)
+        n3_sb = load_list("n3_sb", n3)
+        n4_sb = load_list("n4_sb", n4)
+
+        d_plane = tile("d_plane", H, U8)
+        nc.vector.memset(d_plane[:].bitcast(I32), 0)
+        y_win = [tile(f"y_win{t}", 2 * S, F32) for t in range(PACK)]
+        for t in range(PACK):
+            nc.vector.memset(y_win[t][:, S:], 0.0)
+
+        gain_abs = tile("gain_abs", PACK, F32)
+        nc.vector.scalar_tensor_tensor(gain_abs[:], gain[:], -1.0, gain[:], ALU.mult, ALU.max)
+        gain_neg = tile("gain_neg", PACK, F32)
+        nc.vector.tensor_scalar(gain_neg[:], gain[:], 0.0, None, ALU.is_lt)
+        signs = tile("signs", PIECE * PACK, BF16)
+        nc.vector.tensor_scalar(
+            signs[:].rearrange("p (j t) -> p j t", t=PACK),
+            gain_neg[:].unsqueeze(1).to_broadcast([P, PIECE, PACK]),
+            -2.0, 1.0, ALU.mult, ALU.add,
+        )
+
+        x_plane = tile("x_plane", S, U8)
+        nc.vector.tensor_copy(x_plane[:], xs_table[:].indirect(offs_sb[:]))
+        ds_picked = tile("ds_picked", H, U8)
+        nc.vector.tensor_copy(ds_picked[:], ds_table[:].indirect(k1_sb[:]))
+
+        w_by_col = w_raw[:].rearrange("p (j m t) -> p m j t", j=PACK, t=PACK)
+        w_bf = [tile(f"w_bf{u}", 2 * H, BF16) for u in range(2)]
+        w_views = [w_bf[u][:].rearrange("p (t m j) -> p m j t", t=2, j=PACK) for u in range(2)]
+        nc.vector.tensor_copy(w_views[0], w_by_col[:, :, :, 0:2])
+        nc.scalar.copy(w_views[1], w_by_col[:, :, :, 2:4])
+        w_codes = [tile(f"w_codes{t}", P, U32) for t in range(PACK)]
+        w_plane = [tile(f"w_plane{t}", P, U8) for t in range(PACK)]
+        for t in range(PACK):
+            nc.vector.quantize_mx(
+                out=w_codes[t][:].bitcast(FP8X4), scales=w_plane[t][:],
+                in_=w_bf[t // 2][:, (t % 2) * H : (t % 2 + 1) * H],
+            )
+
+        d_table = tile("d_table", G, I32, tag="big")
+        nc.sync.dma_start(d_table[:], d_words[0].rearrange("p n t -> p (n t)").bitcast(I32))
+        for q in range(4):
+            nc.sync.dma_start(d_plane[32 * q : 32 * q + 4, :].bitcast(I32), ds_picked[32 * q : 32 * q + 32 : 8, :].bitcast(I32))
+
+        x_codes = tile("x_codes", S, U32)
+        nc.vector.tensor_copy(x_codes[:], x_table[:].bitcast(U32).indirect(offs_sb[:]))
+
+        for t in range(PACK):
+            y_acc = psum.tile([P, S], F32, name=f"y_acc{t}")
+            nc.tensor.matmul_mx(
+                out=y_acc[:], lhsT=w_codes[t][:].bitcast(FP8X4), lhsT_scale=w_plane[t][:],
+                rhs=x_codes[:].bitcast(FP8X4), rhs_scale=x_plane[:], start=True, stop=True,
+            )
+            if t == 0:
+                nc.scalar.activation(y_win[t][:, :S], y_acc[:], ACT.Copy, scale=gain_abs[:, t : t + 1])
+            else:
+                nc.vector.tensor_scalar(y_win[t][:, :S], y_acc[:], gain_abs[:, t : t + 1], None, ALU.mult)
+
+        st = tile("st", PACK * S, F32)
+        for t in range(PACK):
+            y_far = tile(f"y_far{t}", S, F32)
+            nc.scalar.activation(y_far[:], y_win[t][:].indirect(n1_sb[:]), ACT.Copy)
+            nc.vector.tensor_tensor(st[:, t * S : (t + 1) * S], y_win[t][:, :S], y_far[:], ALU.max)
+
+        d_codes = [tile(f"d_codes{u}", H // 2, U32) for u in range(2)]
+
+        def gather_d(u):
+            nc.vector.tensor_copy(d_codes[u][:], d_table[:].bitcast(U32).indirect(k1_sb[:, 16 * u : 16 * (u + 1)]))
+
+        gather_d(0)
+
+        z_codes = tile("z_codes", S, U32)
+        z_plane = tile("z_plane", S, U8)
+        h_acc = [psum.tile([P, S], F32, name=f"h_acc{i}") for i in range(4)]
+        h_win = [tile(f"h_win{i}", S, F32) for i in range(4)]
+
+        def product(i, half):
+            cols = slice(half * HALF, (half + 1) * HALF)
+            nc.tensor.matmul_mx(
+                out=h_acc[i][:, cols],
+                lhsT=d_codes[i // 2][:, (i % 2) * P : (i % 2 + 1) * P].bitcast(FP8X4),
+                lhsT_scale=d_plane[:, i * P : (i + 1) * P],
+                rhs=z_codes[:, cols].bitcast(FP8X4), rhs_scale=z_plane[:, cols], start=True, stop=True,
+            )
+
+        def empty_on_scalar(i, cols):
+            nc.scalar.activation(h_win[i][:, cols], h_acc[i][:, cols], ACT.Copy, scale=0.0625)
+
+        def empty_on_vector(i, cols):
+            nc.vector.tensor_scalar(h_win[i][:, cols], h_acc[i][:, cols], 0.0625, None, ALU.mult)
+
+        st_by_row = st[:].rearrange("p (t c a i) -> p c a t i", t=PACK, c=S // PIECE, i=4)
+        for c in range(S // PIECE):
+            st_far = tile(f"st_far{c}", PACK * PIECE, F32)
+            for t in range(PACK):
+                nc.scalar.activation(
+                    st_far[:, t * PIECE : (t + 1) * PIECE],
+                    st[:, t * S : (t + 1) * S].indirect(n2_sb[:, 4 * c : 4 * (c + 1)]), ACT.Copy,
+                )
+            z_mag = tile(f"z_mag{c}", PACK * PIECE, BF16)
+            nc.vector.tensor_tensor(
+                z_mag[:].rearrange("p (a i t) -> p a t i", i=4, t=PACK),
+                st_by_row[:, c], st_far[:].rearrange("p (t a i) -> p a t i", t=PACK, i=4), ALU.min,
+            )
+            z_bf = tile(f"z_bf{c}", PACK * PIECE, BF16)
+            nc.vector.tensor_tensor(z_bf[:], z_mag[:], signs[:], ALU.mult)
+            cols = slice(c * PIECE, (c + 1) * PIECE)
+            nc.vector.quantize_mx(out=z_codes[:, cols].bitcast(FP8X4), scales=z_plane[:, cols], in_=z_bf[:])
+            if c == 1:
+                product(0, 0)
+                product(1, 0)
+
+        empty_on_scalar(0, slice(0, HALF))
+        empty_on_scalar(1, slice(0, HALF))
+        product(0, 1)
+        product(1, 1)
+        empty_on_scalar(0, slice(HALF, S))
+        empty_on_vector(1, slice(HALF, S))
+        gather_d(1)
+        for i in (2, 3):
+            product(i, 0)
+            product(i, 1)
+
+        pair = [tile(f"pair{i}", S, F32) for i in range(4)]
+        rb = [tile(f"rb{i}", W, F32) for i in range(4)]
+        r2 = [tile(f"r2_{i}", W, F32) for i in range(4)]
+        ra = [tile(f"ra{i}", W, F32) for i in range(4)]
+        res = [tile(f"res{i}", S, F32) for i in range(4)]
+
+        def fetch(i):
+            if i >= 2:
+                empty_on_vector(i, slice(0, S))
+            nc.scalar.activation(pair[i][:, :W], h_win[i][:].indirect(n3_sb[:]), ACT.Copy)
+            nc.scalar.activation(pair[i][:, W:], h_win[i][:].indirect(n4_sb[:]), ACT.Copy)
+            nc.vector.scalar_tensor_tensor(rb[i][:], pair[i][:, :W], -0.5, pair[i][:, W:], ALU.mult, ALU.add)
+            sq = tile(f"sq{i}", S, F32)
+            nc.vector.tensor_tensor(sq[:], pair[i][:], pair[i][:], ALU.mult)
+            nc.vector.scalar_tensor_tensor(r2[i][:], sq[:, :W], 0.25, sq[:, W:], ALU.add, ALU.add)
+
+        def put_rb(i):
+            nc.scalar.activation(res[i][:].indirect(n4_sb[:]), rb[i][:], ACT.Copy)
+            nc.scalar.activation(ra[i][:], r2[i][:], ACT.Sqrt)
+
+        def put_ra(i):
+            nc.scalar.activation(res[i][:].indirect(n3_sb[:]), ra[i][:], ACT.Copy)
+            nc.sync.dma_start(out[i * P : (i + 1) * P, :], res[i][:])
+
+        fetch(0)
+        fetch(1)
+        put_rb(0)
+        fetch(2)
+        put_ra(0)
+        put_rb(1)
+        fetch(3)
+        put_ra(1)
+        put_rb(2)
+        put_rb(3)
+        put_ra(2)
+        put_ra(3)

@@ -17,7 +17,6 @@ ACT = mybir.ActivationFunctionType
 
 P = 128
 PACK = 4
-PIECE = 64
 HALF = S // 2
 
 
@@ -27,6 +26,7 @@ def tile_picked_densehopmnpolar_none_p_kernel(
     nc = tc.nc
     with ExitStack() as ctx:
         keep = ctx.enter_context(tc.tile_pool(name="keep", bufs=1))
+        reuse = ctx.enter_context(tc.tile_pool(name="reuse", bufs=1))
         psum = ctx.enter_context(tc.psum_pool(name="psum", bufs=1))
 
         def tile(name, cols, dtype, tag=None):
@@ -37,24 +37,31 @@ def tile_picked_densehopmnpolar_none_p_kernel(
             nc.sync.dma_start(held[:], src)
             return held
 
+        warm_in = tile("warm_in", 1, F32)
+        nc.gpsimd.memset(warm_in[:], 1.0)
+        warm_out = tile("warm_out", 1, F32)
+        nc.scalar.activation(warm_out[:], warm_in[:], ACT.Sqrt)
+
         xs_table = tile("xs_table", T, U8)
         nc.vector.memset(xs_table[:].bitcast(I32), 0)
         ds_table = tile("ds_table", G, U8)
         nc.vector.memset(ds_table[:].bitcast(I32), 0)
 
         offs_sb = load_list("offs_sb", offs)
-        w_raw = tile("w_raw", PACK * H, F32, tag="big")
-        nc.scalar.dma_start(w_raw[:], w1.rearrange("(p j) c -> p (j c)", j=PACK))
-        x_table = tile("x_table", T, I32)
-        nc.scalar.dma_start(x_table[:], x_words[0].rearrange("p n t -> p (n t)").bitcast(I32))
+        w_raw = tile("w_raw", PACK * H, F32)
+        nc.sync.dma_start(w_raw[:], w1.rearrange("(p j) c -> p (j c)", j=PACK))
         for q in range(4):
             nc.sync.dma_start(xs_table[32 * q : 32 * q + 4, :].bitcast(I32), x_scales[0, 4 * q : 4 * q + 4, :].bitcast(I32))
-        gain = tile("gain", PACK, F32)
-        nc.sync.dma_start(gain[:], gs.rearrange("(p t) o -> p (t o)", t=PACK))
         k1_sb = load_list("k1_sb", k1)
         nc.sync.dma_start(ds_table[0:P:8, :].bitcast(I32), d_scales[0].bitcast(I32))
+        x_table = tile("x_table", T, I32)
+        nc.sync.dma_start(x_table[:], x_words[0].rearrange("p n t -> p (n t)").bitcast(I32))
         n1_sb = load_list("n1_sb", n1)
+        d_table = reuse.tile([P, G], I32, name="d_table", align_bytes=64, offset=0)
+        nc.sync.dma_start(d_table[:], d_words[0].rearrange("p n t -> p (n t)").bitcast(I32))
         n2_sb = load_list("n2_sb", n2)
+        gain = tile("gain", PACK, F32)
+        nc.sync.dma_start(gain[:], gs.rearrange("(p t) o -> p (t o)", t=PACK))
         n3_sb = load_list("n3_sb", n3)
         n4_sb = load_list("n4_sb", n4)
 
@@ -64,21 +71,8 @@ def tile_picked_densehopmnpolar_none_p_kernel(
         for t in range(PACK):
             nc.vector.memset(y_win[t][:, S:], 0.0)
 
-        gain_abs = tile("gain_abs", PACK, F32)
-        nc.vector.scalar_tensor_tensor(gain_abs[:], gain[:], -1.0, gain[:], ALU.mult, ALU.max)
-        gain_neg = tile("gain_neg", PACK, F32)
-        nc.vector.tensor_scalar(gain_neg[:], gain[:], 0.0, None, ALU.is_lt)
-        signs = tile("signs", PIECE * PACK, BF16)
-        nc.vector.tensor_scalar(
-            signs[:].rearrange("p (j t) -> p j t", t=PACK),
-            gain_neg[:].unsqueeze(1).to_broadcast([P, PIECE, PACK]),
-            -2.0, 1.0, ALU.mult, ALU.add,
-        )
-
         x_plane = tile("x_plane", S, U8)
         nc.vector.tensor_copy(x_plane[:], xs_table[:].indirect(offs_sb[:]))
-        ds_picked = tile("ds_picked", H, U8)
-        nc.vector.tensor_copy(ds_picked[:], ds_table[:].indirect(k1_sb[:]))
 
         w_by_col = w_raw[:].rearrange("p (j m t) -> p m j t", j=PACK, t=PACK)
         w_bf = [tile(f"w_bf{u}", 2 * H, BF16) for u in range(2)]
@@ -93,13 +87,13 @@ def tile_picked_densehopmnpolar_none_p_kernel(
                 in_=w_bf[t // 2][:, (t % 2) * H : (t % 2 + 1) * H],
             )
 
-        d_table = tile("d_table", G, I32, tag="big")
-        nc.sync.dma_start(d_table[:], d_words[0].rearrange("p n t -> p (n t)").bitcast(I32))
-        for q in range(4):
-            nc.sync.dma_start(d_plane[32 * q : 32 * q + 4, :].bitcast(I32), ds_picked[32 * q : 32 * q + 32 : 8, :].bitcast(I32))
-
         x_codes = tile("x_codes", S, U32)
         nc.vector.tensor_copy(x_codes[:], x_table[:].bitcast(U32).indirect(offs_sb[:]))
+
+        ds_picked = tile("ds_picked", H, U8, tag="x_table")
+        nc.vector.tensor_copy(ds_picked[:], ds_table[:].indirect(k1_sb[:]))
+        for q in range(4):
+            nc.sync.dma_start(d_plane[32 * q : 32 * q + 4, :].bitcast(I32), ds_picked[32 * q : 32 * q + 32 : 8, :].bitcast(I32))
 
         for t in range(PACK):
             y_acc = psum.tile([P, S], F32, name=f"y_acc{t}")
@@ -108,22 +102,22 @@ def tile_picked_densehopmnpolar_none_p_kernel(
                 rhs=x_codes[:].bitcast(FP8X4), rhs_scale=x_plane[:], start=True, stop=True,
             )
             if t == 0:
-                nc.scalar.activation(y_win[t][:, :S], y_acc[:], ACT.Copy, scale=gain_abs[:, t : t + 1])
+                nc.scalar.copy(y_win[t][:, :S], y_acc[:])
             else:
-                nc.vector.tensor_scalar(y_win[t][:, :S], y_acc[:], gain_abs[:, t : t + 1], None, ALU.mult)
+                nc.vector.tensor_copy(y_win[t][:, :S], y_acc[:])
 
-        st = tile("st", PACK * S, F32)
+        st = []
         for t in range(PACK):
+            if t == 0:
+                st.append(tile("st0", S, F32))
+            else:
+                st.append(reuse.tile([P, S], F32, name=f"st{t}", align_bytes=64, offset=4 * S * t))
             y_far = tile(f"y_far{t}", S, F32)
             nc.scalar.activation(y_far[:], y_win[t][:].indirect(n1_sb[:]), ACT.Copy)
-            nc.vector.tensor_tensor(st[:, t * S : (t + 1) * S], y_win[t][:, :S], y_far[:], ALU.max)
-
-        d_codes = [tile(f"d_codes{u}", H // 2, U32) for u in range(2)]
-
-        def gather_d(u):
-            nc.vector.tensor_copy(d_codes[u][:], d_table[:].bitcast(U32).indirect(k1_sb[:, 16 * u : 16 * (u + 1)]))
-
-        gather_d(0)
+            nc.vector.tensor_tensor(st[t][:], y_win[t][:, :S], y_far[:], ALU.max)
+            if t == 0:
+                d_codes = tile("d_codes", H, U32)
+                nc.vector.tensor_copy(d_codes[:], d_table[:].bitcast(U32).indirect(k1_sb[:]))
 
         z_codes = tile("z_codes", S, U32)
         z_plane = tile("z_plane", S, U8)
@@ -134,7 +128,7 @@ def tile_picked_densehopmnpolar_none_p_kernel(
             cols = slice(half * HALF, (half + 1) * HALF)
             nc.tensor.matmul_mx(
                 out=h_acc[i][:, cols],
-                lhsT=d_codes[i // 2][:, (i % 2) * P : (i % 2 + 1) * P].bitcast(FP8X4),
+                lhsT=d_codes[:, i * P : (i + 1) * P].bitcast(FP8X4),
                 lhsT_scale=d_plane[:, i * P : (i + 1) * P],
                 rhs=z_codes[:, cols].bitcast(FP8X4), rhs_scale=z_plane[:, cols], start=True, stop=True,
             )
@@ -145,37 +139,32 @@ def tile_picked_densehopmnpolar_none_p_kernel(
         def empty_on_vector(i, cols):
             nc.vector.tensor_scalar(h_win[i][:, cols], h_acc[i][:, cols], 0.0625, None, ALU.mult)
 
-        st_by_row = st[:].rearrange("p (t c a i) -> p c a t i", t=PACK, c=S // PIECE, i=4)
-        for c in range(S // PIECE):
-            st_far = tile(f"st_far{c}", PACK * PIECE, F32)
+        for half in range(2):
+            cols = slice(half * HALF, (half + 1) * HALF)
+            low = tile(f"low{half}", PACK * HALF, F32, tag=f"y_win{PACK - 1 - half}")
             for t in range(PACK):
-                nc.scalar.activation(
-                    st_far[:, t * PIECE : (t + 1) * PIECE],
-                    st[:, t * S : (t + 1) * S].indirect(n2_sb[:, 4 * c : 4 * (c + 1)]), ACT.Copy,
-                )
-            z_mag = tile(f"z_mag{c}", PACK * PIECE, BF16)
+                st_far = tile(f"st_far{half}_{t}", HALF, F32, tag=f"st_far{t}")
+                nc.scalar.activation(st_far[:], st[t][:].indirect(n2_sb[:, 8 * half : 8 * (half + 1)]), ACT.Copy)
+                nc.vector.tensor_tensor(low[:, t * HALF : (t + 1) * HALF], st[t][:, cols], st_far[:], ALU.min)
+            z_bf = tile(f"z_bf{half}", PACK * HALF, BF16)
             nc.vector.tensor_tensor(
-                z_mag[:].rearrange("p (a i t) -> p a t i", i=4, t=PACK),
-                st_by_row[:, c], st_far[:].rearrange("p (t a i) -> p a t i", t=PACK, i=4), ALU.min,
+                z_bf[:].rearrange("p (a i t) -> p a t i", i=4, t=PACK),
+                low[:].rearrange("p (t a i) -> p a t i", t=PACK, i=4),
+                gain[:].unsqueeze(1).unsqueeze(3).to_broadcast([P, HALF // 4, PACK, 4]),
+                ALU.mult,
             )
-            z_bf = tile(f"z_bf{c}", PACK * PIECE, BF16)
-            nc.vector.tensor_tensor(z_bf[:], z_mag[:], signs[:], ALU.mult)
-            cols = slice(c * PIECE, (c + 1) * PIECE)
             nc.vector.quantize_mx(out=z_codes[:, cols].bitcast(FP8X4), scales=z_plane[:, cols], in_=z_bf[:])
-            if c == 1:
-                product(0, 0)
-                product(1, 0)
+            if half == 0:
+                for i in range(4):
+                    product(i, 0)
 
-        empty_on_scalar(0, slice(0, HALF))
-        empty_on_scalar(1, slice(0, HALF))
-        product(0, 1)
-        product(1, 1)
-        empty_on_scalar(0, slice(HALF, S))
-        empty_on_vector(1, slice(HALF, S))
-        gather_d(1)
-        for i in (2, 3):
-            product(i, 0)
+        for i in range(4):
+            empty_on_scalar(i, slice(0, HALF))
+        for i in range(4):
             product(i, 1)
+        empty_on_scalar(0, slice(HALF, S))
+        for i in range(1, 4):
+            empty_on_vector(i, slice(HALF, S))
 
         pair = [tile(f"pair{i}", S, F32) for i in range(4)]
         rb = [tile(f"rb{i}", W, F32) for i in range(4)]
@@ -184,8 +173,6 @@ def tile_picked_densehopmnpolar_none_p_kernel(
         res = [tile(f"res{i}", S, F32) for i in range(4)]
 
         def fetch(i):
-            if i >= 2:
-                empty_on_vector(i, slice(0, S))
             nc.scalar.activation(pair[i][:, :W], h_win[i][:].indirect(n3_sb[:]), ACT.Copy)
             nc.scalar.activation(pair[i][:, W:], h_win[i][:].indirect(n4_sb[:]), ACT.Copy)
             nc.vector.scalar_tensor_tensor(rb[i][:], pair[i][:, :W], -0.5, pair[i][:, W:], ALU.mult, ALU.add)

from contextlib import ExitStack

import concourse.mybir as mybir

K, T, S, H, G, W = 512, 2048, 256, 512, 2048, 128
FLOPS = 2 * K * H * S + 2 * H * H * S

F32 = mybir.dt.float32
BF16 = mybir.dt.bfloat16
I32 = mybir.dt.int32
U32 = mybir.dt.uint32
U16 = mybir.dt.uint16
U8 = mybir.dt.uint8
FP8X4 = mybir.dt.float8_e4m3fn_x4
ALU = mybir.AluOpType
ACT = mybir.ActivationFunctionType

P = 128
PACK = 4
HALF = S // 2


def tile_picked_densehopmnpolar_none_p_kernel(
    tc, x_words, x_scales, w1, gs, d_words, d_scales, offs, n1, n2, k1, n3, n4, out
):
    nc = tc.nc
    with ExitStack() as ctx:
        keep = ctx.enter_context(tc.tile_pool(name="keep", bufs=1))
        reuse = ctx.enter_context(tc.tile_pool(name="reuse", bufs=1))
        psum = ctx.enter_context(tc.psum_pool(name="psum", bufs=1))

        def tile(name, cols, dtype, tag=None):
            return keep.tile([P, cols], dtype, name=name, tag=tag or name, align_bytes=64)

        def load_list(name, src):
            held = keep.tile([P, src.shape[1]], U16, name=name)
            nc.sync.dma_start(held[:], src)
            return held

        warm_in = tile("warm_in", 1, F32)
        nc.gpsimd.memset(warm_in[:], 1.0)
        warm_out = tile("warm_out", 1, F32)
        nc.scalar.activation(warm_out[:], warm_in[:], ACT.Sqrt)

        xs_table = tile("xs_table", T, U8)
        nc.vector.memset(xs_table[:].bitcast(I32), 0)
        ds_table = tile("ds_table", G, U8)
        nc.vector.memset(ds_table[:].bitcast(I32), 0)

        offs_sb = load_list("offs_sb", offs)
        w_raw = tile("w_raw", PACK * H, F32)
        nc.sync.dma_start(w_raw[:], w1.rearrange("(p j) c -> p (j c)", j=PACK))
        for q in range(4):
            nc.sync.dma_start(xs_table[32 * q : 32 * q + 4, :].bitcast(I32), x_scales[0, 4 * q : 4 * q + 4, :].bitcast(I32))
        k1_sb = load_list("k1_sb", k1)
        nc.sync.dma_start(ds_table[0:P:8, :].bitcast(I32), d_scales[0].bitcast(I32))
        x_table = tile("x_table", T, I32)
        nc.sync.dma_start(x_table[:], x_words[0].rearrange("p n t -> p (n t)").bitcast(I32))
        n1_sb = load_list("n1_sb", n1)
        d_table = reuse.tile([P, G], I32, name="d_table", align_bytes=64, offset=0)
        nc.sync.dma_start(d_table[:], d_words[0].rearrange("p n t -> p (n t)").bitcast(I32))
        n2_sb = load_list("n2_sb", n2)
        gain = tile("gain", PACK, F32)
        nc.sync.dma_start(gain[:], gs.rearrange("(p t) o -> p (t o)", t=PACK))
        n3_sb = load_list("n3_sb", n3)
        n4_sb = load_list("n4_sb", n4)

        d_plane = tile("d_plane", H, U8)
        nc.vector.memset(d_plane[:].bitcast(I32), 0)
        y_win = [tile(f"y_win{t}", 2 * S, F32) for t in range(PACK)]
        for t in range(PACK):
            nc.vector.memset(y_win[t][:, S:], 0.0)

        x_plane = tile("x_plane", S, U8)
        nc.vector.tensor_copy(x_plane[:], xs_table[:].indirect(offs_sb[:]))

        w_by_col = w_raw[:].rearrange("p (j m t) -> p m j t", j=PACK, t=PACK)
        w_bf = [tile(f"w_bf{u}", 2 * H, BF16) for u in range(2)]
        w_views = [w_bf[u][:].rearrange("p (t m j) -> p m j t", t=2, j=PACK) for u in range(2)]
        nc.vector.tensor_copy(w_views[0], w_by_col[:, :, :, 0:2])
        nc.scalar.copy(w_views[1], w_by_col[:, :, :, 2:4])
        w_codes = [tile(f"w_codes{t}", P, U32) for t in range(PACK)]
        w_plane = [tile(f"w_plane{t}", P, U8) for t in range(PACK)]
        for t in range(PACK):
            nc.vector.quantize_mx(
                out=w_codes[t][:].bitcast(FP8X4), scales=w_plane[t][:],
                in_=w_bf[t // 2][:, (t % 2) * H : (t % 2 + 1) * H],
            )

        x_codes = tile("x_codes", S, U32)
        nc.vector.tensor_copy(x_codes[:], x_table[:].bitcast(U32).indirect(offs_sb[:]))

        ds_picked = tile("ds_picked", H, U8, tag="x_table")
        nc.vector.tensor_copy(ds_picked[:], ds_table[:].indirect(k1_sb[:]))
        for q in range(4):
            nc.sync.dma_start(d_plane[32 * q : 32 * q + 4, :].bitcast(I32), ds_picked[32 * q : 32 * q + 32 : 8, :].bitcast(I32))

        for t in range(PACK):
            y_acc = psum.tile([P, S], F32, name=f"y_acc{t}")
            nc.tensor.matmul_mx(
                out=y_acc[:], lhsT=w_codes[t][:].bitcast(FP8X4), lhsT_scale=w_plane[t][:],
                rhs=x_codes[:].bitcast(FP8X4), rhs_scale=x_plane[:], start=True, stop=True,
            )
            if t == 0:
                nc.scalar.copy(y_win[t][:, :S], y_acc[:])
            else:
                nc.vector.tensor_copy(y_win[t][:, :S], y_acc[:])

        st = []
        for t in range(PACK):
            if t == 0:
                st.append(tile("st0", S, F32))
            else:
                st.append(reuse.tile([P, S], F32, name=f"st{t}", align_bytes=64, offset=4 * S * t))
            y_far = tile(f"y_far{t}", S, F32)
            nc.scalar.activation(y_far[:], y_win[t][:].indirect(n1_sb[:]), ACT.Copy)
            nc.vector.tensor_tensor(st[t][:], y_win[t][:, :S], y_far[:], ALU.max)
            if t == 0:
                d_codes = tile("d_codes", H, U32)
                nc.vector.tensor_copy(d_codes[:], d_table[:].bitcast(U32).indirect(k1_sb[:]))

        z_codes = tile("z_codes", S, U32)
        z_plane = tile("z_plane", S, U8)
        h_acc = [psum.tile([P, S], F32, name=f"h_acc{i}") for i in range(4)]
        h_win = [tile(f"h_win{i}", S, F32) for i in range(4)]

        def product(i, half):
            cols = slice(half * HALF, (half + 1) * HALF)
            nc.tensor.matmul_mx(
                out=h_acc[i][:, cols],
                lhsT=d_codes[:, i * P : (i + 1) * P].bitcast(FP8X4),
                lhsT_scale=d_plane[:, i * P : (i + 1) * P],
                rhs=z_codes[:, cols].bitcast(FP8X4), rhs_scale=z_plane[:, cols], start=True, stop=True,
            )

        def empty_on_scalar(i, cols):
            nc.scalar.activation(h_win[i][:, cols], h_acc[i][:, cols], ACT.Copy, scale=0.0625)

        def empty_on_vector(i, cols):
            nc.vector.tensor_scalar(h_win[i][:, cols], h_acc[i][:, cols], 0.0625, None, ALU.mult)

        for half in range(2):
            cols = slice(half * HALF, (half + 1) * HALF)
            low = tile(f"low{half}", PACK * HALF, F32, tag=f"y_win{PACK - 1 - half}")
            for t in range(PACK):
                st_far = tile(f"st_far{half}_{t}", HALF, F32, tag=f"st_far{t}")
                nc.scalar.activation(st_far[:], st[t][:].indirect(n2_sb[:, 8 * half : 8 * (half + 1)]), ACT.Copy)
                nc.vector.tensor_tensor(low[:, t * HALF : (t + 1) * HALF], st[t][:, cols], st_far[:], ALU.min)
            z_bf = tile(f"z_bf{half}", PACK * HALF, BF16)
            nc.vector.tensor_tensor(
                z_bf[:].rearrange("p (a i t) -> p a t i", i=4, t=PACK),
                low[:].rearrange("p (t a i) -> p a t i", t=PACK, i=4),
                gain[:].unsqueeze(1).unsqueeze(3).to_broadcast([P, HALF // 4, PACK, 4]),
                ALU.mult,
            )
            nc.vector.quantize_mx(out=z_codes[:, cols].bitcast(FP8X4), scales=z_plane[:, cols], in_=z_bf[:])
            if half == 0:
                for i in range(4):
                    product(i, 0)

        for i in range(4):
            empty_on_scalar(i, slice(0, HALF))
        for i in range(4):
            product(i, 1)
        empty_on_scalar(0, slice(HALF, S))
        for i in range(1, 4):
            empty_on_vector(i, slice(HALF, S))

        pair = [tile(f"pair{i}", S, F32) for i in range(4)]
        rb = [tile(f"rb{i}", W, F32) for i in range(4)]
        r2 = [tile(f"r2_{i}", W, F32) for i in range(4)]
        ra = [tile(f"ra{i}", W, F32) for i in range(4)]
        res = [tile(f"res{i}", S, F32) for i in range(4)]

        def fetch(i):
            nc.scalar.activation(pair[i][:, :W], h_win[i][:].indirect(n3_sb[:]), ACT.Copy)
            nc.scalar.activation(pair[i][:, W:], h_win[i][:].indirect(n4_sb[:]), ACT.Copy)
            nc.vector.scalar_tensor_tensor(rb[i][:], pair[i][:, :W], -0.5, pair[i][:, W:], ALU.mult, ALU.add)
            sq = tile(f"sq{i}", S, F32)
            nc.vector.tensor_tensor(sq[:], pair[i][:], pair[i][:], ALU.mult)
            nc.vector.scalar_tensor_tensor(r2[i][:], sq[:, :W], 0.25, sq[:, W:], ALU.add, ALU.add)

        def put_rb(i):
            nc.scalar.activation(res[i][:].indirect(n4_sb[:]), rb[i][:], ACT.Copy)
            nc.scalar.activation(ra[i][:], r2[i][:], ACT.Sqrt)

        def put_ra(i):
            nc.scalar.activation(res[i][:].indirect(n3_sb[:]), ra[i][:], ACT.Copy)
            nc.sync.dma_start(out[i * P : (i + 1) * P, :], res[i][:])

        fetch(0)
        fetch(1)
        put_rb(0)
        fetch(2)
        put_ra(0)
        put_rb(1)
        fetch(3)
        put_ra(1)
        put_rb(2)
        put_rb(3)
        put_ra(2)
        put_ra(3)
